import numpy as np
import ml_dtypes


def mxq(x, axis, fmt="e4m3"):
    dtype, down = {"e4m3": (ml_dtypes.float8_e4m3fn, 7), "e5m2": (ml_dtypes.float8_e5m2, 14)}[fmt]
    v = np.moveaxis(np.asarray(x, np.float32).astype(ml_dtypes.bfloat16).astype(np.float64), axis, -1)
    blocks = v.reshape(v.shape[:-1] + (-1, 32))
    amax = np.abs(blocks).max(-1, keepdims=True)
    byte = np.maximum(np.where(amax > 0, np.frexp(amax)[1] - 1 + 127, 0) - down, 1)
    scale = np.exp2(byte - 127.0)
    codes = (blocks / scale).astype(np.float32).astype(dtype).astype(np.float64)
    return np.moveaxis((codes * scale).reshape(v.shape), -1, axis)


WIDE = False


def mx_kscale(k):
    if not WIDE:
        return np.ones(k)
    levels = np.array([10, -10, 5, -5, 0])
    if k % 512:
        return np.exp2(np.random.permutation(np.resize(levels, k // 32))).repeat(32)
    a = np.empty((k // 512, 16))
    for p in range(k // 512):
        a[p, :8] = np.random.permutation(np.resize(levels, 8))
        for g in range(8):
            far = levels[np.abs(levels - a[p, g]) >= 10]
            a[p, g + 8] = far[np.random.randint(len(far))]
    return np.exp2(a.ravel()).repeat(32)


def f64(x):
    return np.asarray(x).astype(np.float64)


def striped(idx):
    return np.tile(np.asarray(idx).reshape(-1, 16).T, (8, 1)).astype(np.uint16)


def unstriped(offs):
    return offs[:16].T.reshape(-1).astype(np.int64)


B, N, T, D, DV, NQ = 2, 512, 2048, 512, 256, 256
PAGE = 32
CAP = 2.0


def setup_inputs():
    n = np.random.standard_normal
    pages = np.random.permutation(T // PAGE)[:B * N // PAGE]
    idx = (pages[:, None] * PAGE + np.arange(PAGE)[None, :]).reshape(-1)
    s = mx_kscale(D)[:, None]
    u = np.ones(T)
    u[idx] = mx_kscale(B * N)
    r = np.random.uniform(0.5, 2.0, T)
    k = n((D, T)) / s
    v = n((DV, T)) / (u * r)
    return {
        "qT": (n((B, D, NQ)) * s * (1.00 / np.sqrt(D))).astype(np.float32),
        "kT": k.astype(np.float32),
        "vT": v.astype(np.float32),
        "vs": np.tile(u * r, (128, 1)).astype(np.float32),
        "offs": striped(idx),
    }


def reference(qT, kT, vT, vs, offs):
    idx = unstriped(offs)
    k = f64(kT)
    v = f64(vT)
    pick = lambda x: x[:, idx].reshape(x.shape[0], B, N).transpose(1, 0, 2)
    q = f64(qT)
    score = mxq(q, 1, "e4m3").transpose(0, 2, 1) @ mxq(pick(k), 1, "e4m3")
    score = CAP * np.tanh(score / CAP)
    m = score.max(-1, keepdims=True)
    p = np.exp(score - m)
    total = p.sum(-1, keepdims=True)
    w = p * pick(f64(vs))[:, :1, :]
    y = mxq(w, 2, "e4m3") @ mxq(pick(v).transpose(0, 2, 1), 1, "e4m3")
    y = y / total
    return y

@@ -1,0 +1,166 @@
+from contextlib import ExitStack
+
+import concourse.mybir as mybir
+from concourse.masks import make_identity
+
+B, N, T, D, DV, NQ = 2, 512, 2048, 512, 256, 256
+P = 128
+PACK = 4
+CAP = 2.0
+QT = NQ // P
+VB = DV // P
+COLS = N // 16
+
+FLOPS = 2 * B * NQ * N * (D + DV)
+BYTES = 4 * (B * D * NQ + D * T + DV * T + T + B * NQ * DV) + 2 * P * B * COLS
+
+F32 = mybir.dt.float32
+BF16 = mybir.dt.bfloat16
+U32 = mybir.dt.uint32
+U16 = mybir.dt.uint16
+U8 = mybir.dt.uint8
+FP8X4 = mybir.dt.float8_e4m3fn_x4
+ACT = mybir.ActivationFunctionType
+ALU = mybir.AluOpType
+
+
+def tile_attend_gqa_cap_kernel(tc, qT, kT, vT, vs, offs, out):
+    nc = tc.nc
+    with ExitStack() as ctx:
+        keep = ctx.enter_context(tc.tile_pool(name="keep", bufs=1))
+        work = ctx.enter_context(tc.tile_pool(name="work", bufs=4))
+        psum = ctx.enter_context(tc.psum_pool(name="psum", bufs=2))
+
+        offsets = keep.tile([P, B * COLS], U16, name="offsets")
+        k_pool = [keep.tile([P, T], F32, name=f"k_pool{t}") for t in range(PACK)]
+        v_pool = [keep.tile([P, T], F32, name=f"v_pool{h}") for h in range(VB)]
+        q_raw = [keep.tile([P, PACK, NQ], F32, name=f"q_raw{b}") for b in range(B)]
+        vs_pool = keep.tile([P, T], F32, name="vs_pool")
+        ident = keep.tile([P, P], F32, name="ident")
+        warm = keep.tile([P, 1], F32, name="warm")
+
+        nc.sync.dma_start(offsets[:], offs)
+        k_rows = kT.rearrange("(p j) n -> j p n", j=PACK)
+        q_rows = [qT[b].rearrange("(p j) n -> p j n", j=PACK) for b in range(B)]
+        nc.sync.dma_start(k_pool[0][:], k_rows[0])
+        nc.vector.memset(vs_pool[:], 0.0)
+        nc.sync.dma_start(vs_pool[0:1, :], vs[0:1, :])
+        nc.sync.dma_start(k_pool[1][:], k_rows[1])
+        nc.sync.dma_start(q_raw[0][:], q_rows[0])
+        nc.sync.dma_start(k_pool[2][:], k_rows[2])
+        nc.sync.dma_start(k_pool[3][:], k_rows[3])
+        nc.sync.dma_start(q_raw[1][:], q_rows[1])
+        for h in range(VB):
+            nc.sync.dma_start(v_pool[h][:], vT[h * P : (h + 1) * P, :])
+
+        nc.vector.memset(warm[:], 0.0)
+        nc.scalar.activation(warm[:], warm[:], ACT.Exp)
+        make_identity(nc, ident[:])
+
+        vs_row = keep.tile([P, B * N], F32, name="vs_row")
+        nc.vector.tensor_copy(vs_row[:], vs_pool[:].indirect(offsets[:]))
+        vs_all = keep.tile([P, B, N], F32, name="vs_all")
+        vs_col = keep.tile([P, B, PACK], F32, name="vs_col")
+        for b in range(B):
+            up = psum.tile([P, PACK, P], F32, name="turn", bufs=3)
+            for c in range(PACK):
+                nc.tensor.transpose(up[:, c, :], vs_row[:, (b * PACK + c) * P : (b * PACK + c + 1) * P], ident[:])
+            nc.scalar.copy(vs_col[:, b, :], up[:, :, 0])
+        for b in range(B):
+            down = psum.tile([P, PACK, P], F32, name="turn", bufs=3)
+            for c in range(PACK):
+                nc.tensor.transpose(down[:, c, :], vs_col[:, b, c : c + 1].to_broadcast([P, P]), ident[:])
+            nc.scalar.copy(vs_all[:, b, :], down[:].rearrange("p c s -> p (c s)"))
+
+        q_codes, q_scales = [], []
+        for b in range(B):
+            q_packed = keep.tile([P, NQ, PACK], BF16, name=f"q_packed{b}", align_bytes=64)
+            nc.scalar.copy(q_packed[:], q_raw[b][:].rearrange("p j n -> p n j"))
+            codes = keep.tile([P, NQ], U32, name=f"q_codes{b}", align_bytes=64)
+            scales = keep.tile([P, NQ], U8, name=f"q_scales{b}", align_bytes=64)
+            q_codes.append(codes)
+            q_scales.append(scales)
+            nc.vector.quantize_mx(out=codes[:].bitcast(FP8X4), scales=scales[:], in_=q_packed[:].rearrange("p n j -> p (n j)"))
+
+        k_packed = [keep.tile([P, N, PACK], BF16, name=f"k_packed{b}", align_bytes=64) for b in range(B)]
+        k_codes = [keep.tile([P, N], U32, name=f"k_codes{b}", align_bytes=64) for b in range(B)]
+        k_scales = [keep.tile([P, N], U8, name=f"k_scales{b}", align_bytes=64) for b in range(B)]
+        for t in range(PACK - 1):
+            for b in range(B):
+                nc.vector.tensor_copy(k_packed[b][:, :, t], k_pool[t][:].indirect(offsets[:, b * COLS : (b + 1) * COLS]))
+        for b in range(B):
+            t = PACK - 1
+            nc.vector.tensor_copy(k_packed[b][:, :, t], k_pool[t][:].indirect(offsets[:, b * COLS : (b + 1) * COLS]))
+            nc.vector.quantize_mx(out=k_codes[b][:].bitcast(FP8X4), scales=k_scales[b][:], in_=k_packed[b][:].rearrange("p n j -> p (n j)"))
+
+        w_codes, w_scales, inv = {}, {}, {}
+        for b in range(B):
+            for m in range(QT):
+                u = (b, m)
+                cols = slice(m * P, (m + 1) * P)
+                score = psum.tile([P, N], F32, name="score", bufs=3)
+                nc.tensor.matmul_mx(
+                    out=score[:],
+                    lhsT=q_codes[b][:, cols].bitcast(FP8X4),
+                    lhsT_scale=q_scales[b][:, cols],
+                    rhs=k_codes[b][:].bitcast(FP8X4),
+                    rhs_scale=k_scales[b][:],
+                    start=True,
+                    stop=True,
+                )
+                th = work.tile([P, N], F32, name="th")
+                nc.scalar.activation(th[:], score[:], ACT.Tanh, scale=1.0 / CAP)
+                neg = work.tile([P, N], F32, name="neg")
+                low = work.tile([P, 1], F32, name="low")
+                nc.vector.tensor_scalar(neg[:], th[:], -CAP, None, op0=ALU.mult, op1=ALU.min, accum_out=low[:])
+                p = work.tile([P, N], F32, name="p")
+                total = work.tile([P, 1], F32, name="total")
+                nc.scalar.activation(p[:], th[:], ACT.Exp, bias=low[:], scale=CAP, accum_out=total[:])
+                w = work.tile([P, N], BF16, name="w", align_bytes=64)
+                nc.vector.tensor_tensor(w[:], p[:], vs_all[:, b, :], ALU.mult)
+                words = w[:].bitcast(F32)
+                wt = psum.tile([P, 2, P], F32, name="turn", bufs=3)
+                for half in range(2):
+                    nc.tensor.transpose(wt[:, half, :], words[:, half : N // 2 : 2], ident[:])
+                w_packed = work.tile([P, P, PACK], BF16, name="w_packed", align_bytes=64)
+                flat = w_packed[:].rearrange("p n j -> p (n j)")
+                nc.scalar.copy(flat.bitcast(F32).rearrange("p (n h) -> p n h", h=2), wt[:].rearrange("p h n -> p n h"))
+                wc = keep.tile([P, P], U32, name=f"w_codes{b}{m}", align_bytes=64)
+                ws = keep.tile([P, P], U8, name=f"w_scales{b}{m}", align_bytes=64)
+                nc.vector.quantize_mx(out=wc[:].bitcast(FP8X4), scales=ws[:], in_=flat)
+                r = keep.tile([P, 1], F32, name=f"inv{b}{m}")
+                nc.vector.reciprocal(r[:], total[:])
+                w_codes[u], w_scales[u], inv[u] = wc, ws, r
+
+        v_codes = [keep.tile([P, DV], U32, name=f"v_codes{b}", align_bytes=64) for b in range(B)]
+        v_scales = [keep.tile([P, DV], U8, name=f"v_scales{b}", align_bytes=64) for b in range(B)]
+        for h in range(VB):
+            v_rows = keep.tile([P, B * N], F32, name=f"v_rows{h}")
+            nc.vector.tensor_copy(v_rows[:], v_pool[h][:].indirect(offsets[:]))
+            for b in range(B):
+                vt = psum.tile([P, PACK, P], F32, name="turn", bufs=3)
+                for t in range(PACK):
+                    nc.tensor.transpose(vt[:, t, :], v_rows[:, b * N + t : (b + 1) * N : PACK], ident[:])
+                v_packed = work.tile([P, P, PACK], BF16, name="v_packed", align_bytes=64)
+                nc.scalar.copy(v_packed[:], vt[:].rearrange("p t e -> p e t"))
+                cols = slice(h * P, (h + 1) * P)
+                nc.vector.quantize_mx(
+                    out=v_codes[b][:, cols].bitcast(FP8X4), scales=v_scales[b][:, cols], in_=v_packed[:].rearrange("p e t -> p (e t)")
+                )
+
+        for b in range(B):
+            for m in range(QT):
+                u = (b, m)
+                y = psum.tile([P, DV], F32, name="y", bufs=2)
+                nc.tensor.matmul_mx(
+                    out=y[:],
+                    lhsT=w_codes[u][:].bitcast(FP8X4),
+                    lhsT_scale=w_scales[u][:],
+                    rhs=v_codes[b][:].bitcast(FP8X4),
+                    rhs_scale=v_scales[b][:],
+                    start=True,
+                    stop=True,
+                )
+                res = work.tile([P, DV], F32, name="res")
+                nc.scalar.activation(res[:], y[:], ACT.Copy, scale=inv[u][:])
+                nc.sync.dma_start(out[b, m * P : (m + 1) * P, :], res[:])

@@ -42,13 +42,12 @@ def tile_attend_gqa_cap_kernel(tc, qT, kT, vT, vs, offs, out):
         nc.sync.dma_start(offsets[:], offs)
         k_rows = kT.rearrange("(p j) n -> j p n", j=PACK)
         q_rows = [qT[b].rearrange("(p j) n -> p j n", j=PACK) for b in range(B)]
-        nc.sync.dma_start(k_pool[0][:], k_rows[0])
-        nc.vector.memset(vs_pool[:], 0.0)
-        nc.sync.dma_start(vs_pool[0:1, :], vs[0:1, :])
-        nc.sync.dma_start(k_pool[1][:], k_rows[1])
+        nc.vector.memset(vs_pool[:, 0 : T // 2], 0.0)
+        nc.gpsimd.memset(vs_pool[:, T // 2 : T], 0.0)
         nc.sync.dma_start(q_raw[0][:], q_rows[0])
-        nc.sync.dma_start(k_pool[2][:], k_rows[2])
-        nc.sync.dma_start(k_pool[3][:], k_rows[3])
+        nc.sync.dma_start(vs_pool[0:1, :], vs[0:1, :])
+        for t in range(PACK):
+            nc.sync.dma_start(k_pool[t][:], k_rows[t])
         nc.sync.dma_start(q_raw[1][:], q_rows[1])
         for h in range(VB):
             nc.sync.dma_start(v_pool[h][:], vT[h * P : (h + 1) * P, :])
@@ -85,12 +84,16 @@ def tile_attend_gqa_cap_kernel(tc, qT, kT, vT, vs, offs, out):
         k_packed = [keep.tile([P, N, PACK], BF16, name=f"k_packed{b}", align_bytes=64) for b in range(B)]
         k_codes = [keep.tile([P, N], U32, name=f"k_codes{b}", align_bytes=64) for b in range(B)]
         k_scales = [keep.tile([P, N], U8, name=f"k_scales{b}", align_bytes=64) for b in range(B)]
+        k_rows_of = keep.tile([P, PACK, B * N], F32, name="k_rows_of")
         for t in range(PACK - 1):
-            for b in range(B):
-                nc.vector.tensor_copy(k_packed[b][:, :, t], k_pool[t][:].indirect(offsets[:, b * COLS : (b + 1) * COLS]))
+            nc.vector.tensor_copy(k_rows_of[:, t, :], k_pool[t][:].indirect(offsets[:]))
+            if t == 1:
+                for b in range(B):
+                    nc.scalar.copy(k_packed[b][:, :, 0:2], k_rows_of[:, 0:2, b * N : (b + 1) * N].rearrange("p j n -> p n j"))
         for b in range(B):
-            t = PACK - 1
-            nc.vector.tensor_copy(k_packed[b][:, :, t], k_pool[t][:].indirect(offsets[:, b * COLS : (b + 1) * COLS]))
+            own = slice(b * N, (b + 1) * N)
+            nc.vector.tensor_copy(k_rows_of[:, 3, own], k_pool[3][:].indirect(offsets[:, b * COLS : (b + 1) * COLS]))
+            nc.vector.tensor_copy(k_packed[b][:, :, 2:4], k_rows_of[:, 2:4, own].rearrange("p j n -> p n j"))
             nc.vector.quantize_mx(out=k_codes[b][:].bitcast(FP8X4), scales=k_scales[b][:], in_=k_packed[b][:].rearrange("p n j -> p (n j)"))
 
         w_codes, w_scales, inv = {}, {}, {}
@@ -162,5 +165,8 @@ def tile_attend_gqa_cap_kernel(tc, qT, kT, vT, vs, offs, out):
                     stop=True,
                 )
                 res = work.tile([P, DV], F32, name="res")
-                nc.scalar.activation(res[:], y[:], ACT.Copy, scale=inv[u][:])
+                if m == 0:
+                    nc.vector.tensor_scalar(res[:], y[:], inv[u][:], None, op0=ALU.mult)
+                else:
+                    nc.scalar.activation(res[:], y[:], ACT.Copy, scale=inv[u][:])
                 nc.sync.dma_start(out[b, m * P : (m + 1) * P, :], res[:])

@@ -36,137 +36,224 @@ def tile_attend_gqa_cap_kernel(tc, qT, kT, vT, vs, offs, out):
         v_pool = [keep.tile([P, T], F32, name=f"v_pool{h}") for h in range(VB)]
         q_raw = [keep.tile([P, PACK, NQ], F32, name=f"q_raw{b}") for b in range(B)]
         vs_pool = keep.tile([P, T], F32, name="vs_pool")
+        vs_row = keep.tile([P, B * N], F32, name="vs_row")
+        vs_col = keep.tile([P, B, PACK], F32, name="vs_col")
         ident = keep.tile([P, P], F32, name="ident")
         warm = keep.tile([P, 1], F32, name="warm")
+        totals = keep.tile([P, B * QT], F32, name="totals")
+        inv = keep.tile([P, B * QT], F32, name="inv")
+        q_packed = [keep.tile([P, NQ, PACK], BF16, name=f"q_packed{b}", align_bytes=64) for b in range(B)]
+        q_codes = [keep.tile([P, NQ], U32, name=f"q_codes{b}", align_bytes=64) for b in range(B)]
+        q_scales = [keep.tile([P, NQ], U8, name=f"q_scales{b}", align_bytes=64) for b in range(B)]
+        k_rows_of = keep.tile([P, PACK, B * N], F32, name="k_rows_of")
+        k_packed = [keep.tile([P, N, PACK], BF16, name=f"k_packed{b}", align_bytes=64) for b in range(B)]
+        k_codes = [keep.tile([P, N], U32, name=f"k_codes{b}", align_bytes=64) for b in range(B)]
+        k_scales = [keep.tile([P, N], U8, name=f"k_scales{b}", align_bytes=64) for b in range(B)]
+        v_rows = [keep.tile([P, B * N], F32, name=f"v_rows{h}") for h in range(VB)]
+        v_packed = [keep.tile([P, DV, PACK], BF16, name=f"v_packed{b}", align_bytes=64) for b in range(B)]
+        v_codes = [keep.tile([P, DV], U32, name=f"v_codes{b}", align_bytes=64) for b in range(B)]
+        v_scales = [keep.tile([P, DV], U8, name=f"v_scales{b}", align_bytes=64) for b in range(B)]
+        units = [(b, m) for b in range(B) for m in range(QT)]
+        w_codes = {u: keep.tile([P, P], U32, name=f"w_codes{u[0]}{u[1]}", align_bytes=64) for u in units}
+        w_scales = {u: keep.tile([P, P], U8, name=f"w_scales{u[0]}{u[1]}", align_bytes=64) for u in units}
+        w_packed = {u: keep.tile([P, P, PACK], BF16, name=f"w_packed{u[0]}{u[1]}", align_bytes=64) for u in units}
+        th = {u: keep.tile([P, N], F32, name=f"th{u[0]}{u[1]}") for u in units}
+        low = {u: keep.tile([P, 1], F32, name=f"low{u[0]}{u[1]}") for u in units}
+        p = {u: keep.tile([P, PACK, P], F32, name=f"p{u[0]}{u[1]}") for u in units}
+        score, wt, vt = {}, {}, {}
 
+        def quant(codes, scales, packed):
+            nc.vector.quantize_mx(out=codes.bitcast(FP8X4), scales=scales, in_=packed.rearrange("p n j -> p (n j)"))
+
+        def interleave_q(b):
+            nc.scalar.copy(q_packed[b][:], q_raw[b][:].rearrange("p j n -> p n j"))
+
+        def quant_q(b):
+            quant(q_codes[b][:], q_scales[b][:], q_packed[b][:])
+
+        def gather_vs():
+            nc.vector.tensor_copy(vs_row[:], vs_pool[:].indirect(offsets[:]))
+
+        def turn_vs():
+            for b in range(B):
+                up = psum.tile([P, PACK, P], F32, name="turn", bufs=4)
+                for t in range(PACK):
+                    nc.tensor.transpose(up[:, t, :], vs_row[:, b * N + t : (b + 1) * N : PACK], ident[:])
+                nc.scalar.copy(vs_col[:, b, :], up[:, :, 0])
+
+        def gather_k(t):
+            nc.vector.tensor_copy(k_rows_of[:, t, :], k_pool[t][:].indirect(offsets[:]))
+
+        def gather_k_of(t, b):
+            nc.vector.tensor_copy(k_rows_of[:, t, b * N : (b + 1) * N], k_pool[t][:].indirect(offsets[:, b * COLS : (b + 1) * COLS]))
+
+        def interleave_k(copy, t, b):
+            copy(k_packed[b][:, :, t : t + 2], k_rows_of[:, t : t + 2, b * N : (b + 1) * N].rearrange("p j n -> p n j"))
+
+        def quant_k(b):
+            quant(k_codes[b][:], k_scales[b][:], k_packed[b][:])
+
+        def scores(b, m):
+            cols = slice(m * P, (m + 1) * P)
+            s = psum.tile([P, N], F32, name="score", bufs=2)
+            score[b, m] = s
+            nc.tensor.matmul_mx(
+                out=s[:],
+                lhsT=q_codes[b][:, cols].bitcast(FP8X4),
+                lhsT_scale=q_scales[b][:, cols],
+                rhs=k_codes[b][:].bitcast(FP8X4),
+                rhs_scale=k_scales[b][:],
+                start=True,
+                stop=True,
+            )
+
+        def squash(*u):
+            nc.scalar.activation(th[u][:], score[u][:], ACT.Tanh, scale=1.0 / CAP)
+
+        def lowest(*u):
+            neg = work.tile([P, N], F32, name="neg")
+            nc.vector.tensor_scalar(neg[:], th[u][:], -CAP, None, op0=ALU.mult, op1=ALU.min, accum_out=low[u][:])
+
+        def expo(*u):
+            i = units.index(u)
+            nc.scalar.activation(
+                p[u][:].rearrange("q t s -> q s t"),
+                th[u][:].rearrange("q (s t) -> q s t", t=PACK),
+                ACT.Exp,
+                bias=low[u][:],
+                scale=CAP,
+                accum_out=totals[:, i : i + 1],
+            )
+
+        def turn_w(*u):
+            x = psum.tile([P, PACK, P], F32, name="turn", bufs=4)
+            wt[u] = x
+            for t in range(PACK):
+                nc.tensor.transpose(x[:, t, :], p[u][:, t, :], ident[:])
+
+        def weigh(*u):
+            nc.vector.tensor_tensor(
+                w_packed[u][:],
+                wt[u][:].rearrange("p t q -> p q t"),
+                vs_col[:, u[0], :].unsqueeze(1).to_broadcast([P, P, PACK]),
+                ALU.mult,
+            )
+
+        def quant_w(*u):
+            quant(w_codes[u][:], w_scales[u][:], w_packed[u][:])
+
+        def gather_v(h):
+            nc.vector.tensor_copy(v_rows[h][:], v_pool[h][:].indirect(offsets[:]))
+
+        def turn_v(h, b):
+            x = psum.tile([P, PACK, P], F32, name="turn", bufs=4)
+            vt[h, b] = x
+            for t in range(PACK):
+                nc.tensor.transpose(x[:, t, :], v_rows[h][:, b * N + t : (b + 1) * N : PACK], ident[:])
+
+        def pack_v(h, b):
+            nc.scalar.copy(v_packed[b][:, h * P : (h + 1) * P, :], vt[h, b][:].rearrange("p t e -> p e t"))
+
+        def quant_v(b):
+            quant(v_codes[b][:], v_scales[b][:], v_packed[b][:])
+
+        def finish(b, m, scalar):
+            u = (b, m)
+            i = units.index(u)
+            y = psum.tile([P, DV], F32, name="y", bufs=2)
+            nc.tensor.matmul_mx(
+                out=y[:],
+                lhsT=w_codes[u][:].bitcast(FP8X4),
+                lhsT_scale=w_scales[u][:],
+                rhs=v_codes[b][:].bitcast(FP8X4),
+                rhs_scale=v_scales[b][:],
+                start=True,
+                stop=True,
+            )
+            res = work.tile([P, DV], F32, name="res")
+            if scalar:
+                nc.scalar.activation(res[:], y[:], ACT.Copy, scale=inv[:, i : i + 1])
+            else:
+                nc.vector.tensor_scalar(res[:], y[:], inv[:, i : i + 1], None, op0=ALU.mult)
+            nc.sync.dma_start(out[b, m * P : (m + 1) * P, :], res[:])
+
+        nc.gpsimd.memset(vs_pool[:, T // 2 : T], 0.0)
+        nc.vector.memset(vs_pool[:, 0 : T // 2], 0.0)
         nc.sync.dma_start(offsets[:], offs)
         k_rows = kT.rearrange("(p j) n -> j p n", j=PACK)
         q_rows = [qT[b].rearrange("(p j) n -> p j n", j=PACK) for b in range(B)]
-        nc.vector.memset(vs_pool[:, 0 : T // 2], 0.0)
-        nc.gpsimd.memset(vs_pool[:, T // 2 : T], 0.0)
-        nc.sync.dma_start(q_raw[0][:], q_rows[0])
+        nc.sync.dma_start(k_pool[0][:], k_rows[0])
         nc.sync.dma_start(vs_pool[0:1, :], vs[0:1, :])
-        for t in range(PACK):
-            nc.sync.dma_start(k_pool[t][:], k_rows[t])
+        nc.sync.dma_start(k_pool[1][:], k_rows[1])
+        nc.sync.dma_start(q_raw[0][:], q_rows[0])
+        nc.sync.dma_start(k_pool[2][:], k_rows[2])
+        nc.sync.dma_start(k_pool[3][:], k_rows[3])
         nc.sync.dma_start(q_raw[1][:], q_rows[1])
-        for h in range(VB):
-            nc.sync.dma_start(v_pool[h][:], vT[h * P : (h + 1) * P, :])
-
+        nc.sync.dma_start(v_pool[0][:], vT[0:128, :])
+        nc.sync.dma_start(v_pool[1][:], vT[128:256, :])
         nc.vector.memset(warm[:], 0.0)
         nc.scalar.activation(warm[:], warm[:], ACT.Exp)
         make_identity(nc, ident[:])
 
-        vs_row = keep.tile([P, B * N], F32, name="vs_row")
-        nc.vector.tensor_copy(vs_row[:], vs_pool[:].indirect(offsets[:]))
-        vs_all = keep.tile([P, B, N], F32, name="vs_all")
-        vs_col = keep.tile([P, B, PACK], F32, name="vs_col")
-        for b in range(B):
-            up = psum.tile([P, PACK, P], F32, name="turn", bufs=3)
-            for c in range(PACK):
-                nc.tensor.transpose(up[:, c, :], vs_row[:, (b * PACK + c) * P : (b * PACK + c + 1) * P], ident[:])
-            nc.scalar.copy(vs_col[:, b, :], up[:, :, 0])
-        for b in range(B):
-            down = psum.tile([P, PACK, P], F32, name="turn", bufs=3)
-            for c in range(PACK):
-                nc.tensor.transpose(down[:, c, :], vs_col[:, b, c : c + 1].to_broadcast([P, P]), ident[:])
-            nc.scalar.copy(vs_all[:, b, :], down[:].rearrange("p c s -> p (c s)"))
-
-        q_codes, q_scales = [], []
-        for b in range(B):
-            q_packed = keep.tile([P, NQ, PACK], BF16, name=f"q_packed{b}", align_bytes=64)
-            nc.scalar.copy(q_packed[:], q_raw[b][:].rearrange("p j n -> p n j"))
-            codes = keep.tile([P, NQ], U32, name=f"q_codes{b}", align_bytes=64)
-            scales = keep.tile([P, NQ], U8, name=f"q_scales{b}", align_bytes=64)
-            q_codes.append(codes)
-            q_scales.append(scales)
-            nc.vector.quantize_mx(out=codes[:].bitcast(FP8X4), scales=scales[:], in_=q_packed[:].rearrange("p n j -> p (n j)"))
-
-        k_packed = [keep.tile([P, N, PACK], BF16, name=f"k_packed{b}", align_bytes=64) for b in range(B)]
-        k_codes = [keep.tile([P, N], U32, name=f"k_codes{b}", align_bytes=64) for b in range(B)]
-        k_scales = [keep.tile([P, N], U8, name=f"k_scales{b}", align_bytes=64) for b in range(B)]
-        k_rows_of = keep.tile([P, PACK, B * N], F32, name="k_rows_of")
-        for t in range(PACK - 1):
-            nc.vector.tensor_copy(k_rows_of[:, t, :], k_pool[t][:].indirect(offsets[:]))
-            if t == 1:
-                for b in range(B):
-                    nc.scalar.copy(k_packed[b][:, :, 0:2], k_rows_of[:, 0:2, b * N : (b + 1) * N].rearrange("p j n -> p n j"))
-        for b in range(B):
-            own = slice(b * N, (b + 1) * N)
-            nc.vector.tensor_copy(k_rows_of[:, 3, own], k_pool[3][:].indirect(offsets[:, b * COLS : (b + 1) * COLS]))
-            nc.vector.tensor_copy(k_packed[b][:, :, 2:4], k_rows_of[:, 2:4, own].rearrange("p j n -> p n j"))
-            nc.vector.quantize_mx(out=k_codes[b][:].bitcast(FP8X4), scales=k_scales[b][:], in_=k_packed[b][:].rearrange("p n j -> p (n j)"))
-
-        w_codes, w_scales, inv = {}, {}, {}
-        for b in range(B):
-            for m in range(QT):
-                u = (b, m)
-                cols = slice(m * P, (m + 1) * P)
-                score = psum.tile([P, N], F32, name="score", bufs=3)
-                nc.tensor.matmul_mx(
-                    out=score[:],
-                    lhsT=q_codes[b][:, cols].bitcast(FP8X4),
-                    lhsT_scale=q_scales[b][:, cols],
-                    rhs=k_codes[b][:].bitcast(FP8X4),
-                    rhs_scale=k_scales[b][:],
-                    start=True,
-                    stop=True,
-                )
-                th = work.tile([P, N], F32, name="th")
-                nc.scalar.activation(th[:], score[:], ACT.Tanh, scale=1.0 / CAP)
-                neg = work.tile([P, N], F32, name="neg")
-                low = work.tile([P, 1], F32, name="low")
-                nc.vector.tensor_scalar(neg[:], th[:], -CAP, None, op0=ALU.mult, op1=ALU.min, accum_out=low[:])
-                p = work.tile([P, N], F32, name="p")
-                total = work.tile([P, 1], F32, name="total")
-                nc.scalar.activation(p[:], th[:], ACT.Exp, bias=low[:], scale=CAP, accum_out=total[:])
-                w = work.tile([P, N], BF16, name="w", align_bytes=64)
-                nc.vector.tensor_tensor(w[:], p[:], vs_all[:, b, :], ALU.mult)
-                words = w[:].bitcast(F32)
-                wt = psum.tile([P, 2, P], F32, name="turn", bufs=3)
-                for half in range(2):
-                    nc.tensor.transpose(wt[:, half, :], words[:, half : N // 2 : 2], ident[:])
-                w_packed = work.tile([P, P, PACK], BF16, name="w_packed", align_bytes=64)
-                flat = w_packed[:].rearrange("p n j -> p (n j)")
-                nc.scalar.copy(flat.bitcast(F32).rearrange("p (n h) -> p n h", h=2), wt[:].rearrange("p h n -> p n h"))
-                wc = keep.tile([P, P], U32, name=f"w_codes{b}{m}", align_bytes=64)
-                ws = keep.tile([P, P], U8, name=f"w_scales{b}{m}", align_bytes=64)
-                nc.vector.quantize_mx(out=wc[:].bitcast(FP8X4), scales=ws[:], in_=flat)
-                r = keep.tile([P, 1], F32, name=f"inv{b}{m}")
-                nc.vector.reciprocal(r[:], total[:])
-                w_codes[u], w_scales[u], inv[u] = wc, ws, r
-
-        v_codes = [keep.tile([P, DV], U32, name=f"v_codes{b}", align_bytes=64) for b in range(B)]
-        v_scales = [keep.tile([P, DV], U8, name=f"v_scales{b}", align_bytes=64) for b in range(B)]
-        for h in range(VB):
-            v_rows = keep.tile([P, B * N], F32, name=f"v_rows{h}")
-            nc.vector.tensor_copy(v_rows[:], v_pool[h][:].indirect(offsets[:]))
-            for b in range(B):
-                vt = psum.tile([P, PACK, P], F32, name="turn", bufs=3)
-                for t in range(PACK):
-                    nc.tensor.transpose(vt[:, t, :], v_rows[:, b * N + t : (b + 1) * N : PACK], ident[:])
-                v_packed = work.tile([P, P, PACK], BF16, name="v_packed", align_bytes=64)
-                nc.scalar.copy(v_packed[:], vt[:].rearrange("p t e -> p e t"))
-                cols = slice(h * P, (h + 1) * P)
-                nc.vector.quantize_mx(
-                    out=v_codes[b][:, cols].bitcast(FP8X4), scales=v_scales[b][:, cols], in_=v_packed[:].rearrange("p e t -> p (e t)")
-                )
-
-        for b in range(B):
-            for m in range(QT):
-                u = (b, m)
-                y = psum.tile([P, DV], F32, name="y", bufs=2)
-                nc.tensor.matmul_mx(
-                    out=y[:],
-                    lhsT=w_codes[u][:].bitcast(FP8X4),
-                    lhsT_scale=w_scales[u][:],
-                    rhs=v_codes[b][:].bitcast(FP8X4),
-                    rhs_scale=v_scales[b][:],
-                    start=True,
-                    stop=True,
-                )
-                res = work.tile([P, DV], F32, name="res")
-                if m == 0:
-                    nc.vector.tensor_scalar(res[:], y[:], inv[u][:], None, op0=ALU.mult)
-                else:
-                    nc.scalar.activation(res[:], y[:], ACT.Copy, scale=inv[u][:])
-                nc.sync.dma_start(out[b, m * P : (m + 1) * P, :], res[:])
+        gather_k(0)
+        gather_vs()
+        turn_vs()
+        gather_k(1)
+        interleave_q(0)
+        interleave_k(nc.vector.tensor_copy, 0, 0)
+        interleave_k(nc.vector.tensor_copy, 0, 1)
+        quant_q(0)
+        gather_k(2)
+        gather_k_of(3, 1)
+        gather_k_of(3, 0)
+        interleave_k(nc.scalar.copy, 2, 1)
+        interleave_k(nc.vector.tensor_copy, 2, 0)
+        quant_k(0)
+        interleave_q(1)
+        scores(0, 0)
+        scores(0, 1)
+        squash(0, 0)
+        squash(0, 1)
+        quant_k(1)
+        gather_v(0)
+        quant_q(1)
+        scores(1, 0)
+        scores(1, 1)
+        turn_v(0, 0)
+        turn_v(0, 1)
+        lowest(0, 0)
+        lowest(0, 1)
+        expo(0, 0)
+        squash(1, 0)
+        expo(0, 1)
+        gather_v(1)
+        turn_w(0, 0)
+        squash(1, 1)
+        lowest(1, 0)
+        turn_w(0, 1)
+        pack_v(0, 0)
+        lowest(1, 1)
+        expo(1, 0)
+        weigh(0, 0)
+        expo(1, 1)
+        weigh(0, 1)
+        quant_w(0, 0)
+        turn_w(1, 0)
+        quant_w(0, 1)
+        pack_v(0, 1)
+        turn_v(1, 0)
+        turn_w(1, 1)
+        pack_v(1, 0)
+        weigh(1, 0)
+        turn_v(1, 1)
+        weigh(1, 1)
+        pack_v(1, 1)
+        quant_w(1, 0)
+        quant_v(0)
+        nc.vector.reciprocal(inv[:], totals[:])
+        finish(0, 0, False)
+        finish(0, 1, True)
+        quant_w(1, 1)
+        quant_v(1)
+        finish(1, 0, False)
+        finish(1, 1, True)

@@ -60,13 +60,14 @@ def tile_attend_gqa_cap_kernel(tc, qT, kT, vT, vs, offs, out):
         th = {u: keep.tile([P, N], F32, name=f"th{u[0]}{u[1]}") for u in units}
         low = {u: keep.tile([P, 1], F32, name=f"low{u[0]}{u[1]}") for u in units}
         p = {u: keep.tile([P, PACK, P], F32, name=f"p{u[0]}{u[1]}") for u in units}
-        score, wt, vt = {}, {}, {}
+        score, wt, vt, acc = {}, {}, {}, {}
+        over = {(0, 1): "v_pool0"}
 
         def quant(codes, scales, packed):
             nc.vector.quantize_mx(out=codes.bitcast(FP8X4), scales=scales, in_=packed.rearrange("p n j -> p (n j)"))
 
-        def interleave_q(b):
-            nc.scalar.copy(q_packed[b][:], q_raw[b][:].rearrange("p j n -> p n j"))
+        def interleave_q(copy, b):
+            copy(q_packed[b][:], q_raw[b][:].rearrange("p j n -> p n j"))
 
         def quant_q(b):
             quant(q_codes[b][:], q_scales[b][:], q_packed[b][:])
@@ -111,7 +112,10 @@ def tile_attend_gqa_cap_kernel(tc, qT, kT, vT, vs, offs, out):
             nc.scalar.activation(th[u][:], score[u][:], ACT.Tanh, scale=1.0 / CAP)
 
         def lowest(*u):
-            neg = work.tile([P, N], F32, name="neg")
+            if u in over:
+                neg = keep.tile([P, N], F32, name=f"neg{u[0]}{u[1]}", tag=over[u])
+            else:
+                neg = work.tile([P, N], F32, name="neg")
             nc.vector.tensor_scalar(neg[:], th[u][:], -CAP, None, op0=ALU.mult, op1=ALU.min, accum_out=low[u][:])
 
         def expo(*u):
@@ -151,16 +155,16 @@ def tile_attend_gqa_cap_kernel(tc, qT, kT, vT, vs, offs, out):
             for t in range(PACK):
                 nc.tensor.transpose(x[:, t, :], v_rows[h][:, b * N + t : (b + 1) * N : PACK], ident[:])
 
-        def pack_v(h, b):
-            nc.scalar.copy(v_packed[b][:, h * P : (h + 1) * P, :], vt[h, b][:].rearrange("p t e -> p e t"))
+        def pack_v(copy, h, b):
+            copy(v_packed[b][:, h * P : (h + 1) * P, :], vt[h, b][:].rearrange("p t e -> p e t"))
 
         def quant_v(b):
             quant(v_codes[b][:], v_scales[b][:], v_packed[b][:])
 
-        def finish(b, m, scalar):
-            u = (b, m)
-            i = units.index(u)
+        def product(*u):
+            b = u[0]
             y = psum.tile([P, DV], F32, name="y", bufs=2)
+            acc[u] = y
             nc.tensor.matmul_mx(
                 out=y[:],
                 lhsT=w_codes[u][:].bitcast(FP8X4),
@@ -170,6 +174,11 @@ def tile_attend_gqa_cap_kernel(tc, qT, kT, vT, vs, offs, out):
                 start=True,
                 stop=True,
             )
+
+        def finish(b, m, scalar):
+            u = (b, m)
+            i = units.index(u)
+            y = acc[u]
             res = work.tile([P, DV], F32, name="res")
             if scalar:
                 nc.scalar.activation(res[:], y[:], ACT.Copy, scale=inv[:, i : i + 1])
@@ -195,65 +204,69 @@ def tile_attend_gqa_cap_kernel(tc, qT, kT, vT, vs, offs, out):
         nc.scalar.activation(warm[:], warm[:], ACT.Exp)
         make_identity(nc, ident[:])
 
+        gather_v(0)
+        gather_v(1)
         gather_k(0)
-        gather_vs()
-        turn_vs()
-        gather_k(1)
-        interleave_q(0)
-        interleave_k(nc.vector.tensor_copy, 0, 0)
-        interleave_k(nc.vector.tensor_copy, 0, 1)
-        quant_q(0)
         gather_k(2)
-        gather_k_of(3, 1)
+        gather_k(1)
+        gather_vs()
         gather_k_of(3, 0)
-        interleave_k(nc.scalar.copy, 2, 1)
+        interleave_k(nc.scalar.copy, 0, 0)
+        interleave_q(nc.vector.tensor_copy, 0)
+        gather_k_of(3, 1)
+        interleave_k(nc.vector.tensor_copy, 2, 1)
+        quant_q(0)
         interleave_k(nc.vector.tensor_copy, 2, 0)
         quant_k(0)
-        interleave_q(1)
-        scores(0, 0)
-        scores(0, 1)
-        squash(0, 0)
-        squash(0, 1)
-        quant_k(1)
-        gather_v(0)
+        scores(0,1)
+        interleave_q(nc.scalar.copy, 1)
+        turn_vs()
+        interleave_k(nc.vector.tensor_copy, 0, 1)
+        turn_v(0,0)
+        squash(0,1)
         quant_q(1)
-        scores(1, 0)
-        scores(1, 1)
-        turn_v(0, 0)
-        turn_v(0, 1)
-        lowest(0, 0)
-        lowest(0, 1)
-        expo(0, 0)
-        squash(1, 0)
-        expo(0, 1)
-        gather_v(1)
-        turn_w(0, 0)
-        squash(1, 1)
-        lowest(1, 0)
-        turn_w(0, 1)
-        pack_v(0, 0)
-        lowest(1, 1)
-        expo(1, 0)
-        weigh(0, 0)
-        expo(1, 1)
-        weigh(0, 1)
-        quant_w(0, 0)
-        turn_w(1, 0)
-        quant_w(0, 1)
-        pack_v(0, 1)
-        turn_v(1, 0)
-        turn_w(1, 1)
-        pack_v(1, 0)
-        weigh(1, 0)
-        turn_v(1, 1)
-        weigh(1, 1)
-        pack_v(1, 1)
-        quant_w(1, 0)
-        quant_v(0)
+        scores(0,0)
+        squash(0,0)
+        lowest(0,0)
+        quant_k(1)
+        scores(1,0)
+        expo(0,0)
+        pack_v(nc.scalar.copy, 0, 0)
+        lowest(0,1)
+        expo(0,1)
+        squash(1,0)
+        lowest(1,0)
+        turn_v(0,1)
+        expo(1,0)
+        scores(1,1)
+        squash(1,1)
+        lowest(1,1)
+        pack_v(nc.scalar.copy, 0, 1)
+        turn_w(0,0)
+        turn_v(1,0)
+        expo(1,1)
+        turn_w(0,1)
         nc.vector.reciprocal(inv[:], totals[:])
-        finish(0, 0, False)
-        finish(0, 1, True)
-        quant_w(1, 1)
+        turn_w(1,1)
+        weigh(0,0)
+        pack_v(nc.scalar.copy, 1, 0)
+        turn_v(1,1)
+        quant_w(0,0)
+        quant_v(0)
+        pack_v(nc.scalar.copy, 1, 1)
+        weigh(0,1)
+        quant_w(0,1)
+        turn_w(1,0)
+        weigh(1,1)
+        weigh(1,0)
+        product(0,1)
+        product(0,0)
+        quant_w(1,1)
+        finish(0, 0, True)
         quant_v(1)
-        finish(1, 0, False)
-        finish(1, 1, True)
+        finish(0, 1, True)
+        product(1,1)
+        quant_w(1,0)
+        product(1,0)
+        finish(1, 0, True)
+        finish(1, 1, False)

from contextlib import ExitStack

import concourse.mybir as mybir
from concourse.masks import make_identity

B, N, T, D, DV, NQ = 2, 512, 2048, 512, 256, 256
P = 128
PACK = 4
CAP = 2.0
QT = NQ // P
VB = DV // P
COLS = N // 16

FLOPS = 2 * B * NQ * N * (D + DV)
BYTES = 4 * (B * D * NQ + D * T + DV * T + T + B * NQ * DV) + 2 * P * B * COLS

F32 = mybir.dt.float32
BF16 = mybir.dt.bfloat16
U32 = mybir.dt.uint32
U16 = mybir.dt.uint16
U8 = mybir.dt.uint8
FP8X4 = mybir.dt.float8_e4m3fn_x4
ACT = mybir.ActivationFunctionType
ALU = mybir.AluOpType


def tile_attend_gqa_cap_kernel(tc, qT, kT, vT, vs, offs, out):
    nc = tc.nc
    with ExitStack() as ctx:
        keep = ctx.enter_context(tc.tile_pool(name="keep", bufs=1))
        work = ctx.enter_context(tc.tile_pool(name="work", bufs=4))
        psum = ctx.enter_context(tc.psum_pool(name="psum", bufs=2))

        offsets = keep.tile([P, B * COLS], U16, name="offsets")
        k_pool = [keep.tile([P, T], F32, name=f"k_pool{t}") for t in range(PACK)]
        v_pool = [keep.tile([P, T], F32, name=f"v_pool{h}") for h in range(VB)]
        q_raw = [keep.tile([P, PACK, NQ], F32, name=f"q_raw{b}") for b in range(B)]
        vs_pool = keep.tile([P, T], F32, name="vs_pool")
        vs_row = keep.tile([P, B * N], F32, name="vs_row")
        vs_col = keep.tile([P, B, PACK], F32, name="vs_col")
        ident = keep.tile([P, P], F32, name="ident")
        warm = keep.tile([P, 1], F32, name="warm")
        totals = keep.tile([P, B * QT], F32, name="totals")
        inv = keep.tile([P, B * QT], F32, name="inv")
        q_packed = [keep.tile([P, NQ, PACK], BF16, name=f"q_packed{b}", align_bytes=64) for b in range(B)]
        q_codes = [keep.tile([P, NQ], U32, name=f"q_codes{b}", align_bytes=64) for b in range(B)]
        q_scales = [keep.tile([P, NQ], U8, name=f"q_scales{b}", align_bytes=64) for b in range(B)]
        k_rows_of = keep.tile([P, PACK, B * N], F32, name="k_rows_of")
        k_packed = [keep.tile([P, N, PACK], BF16, name=f"k_packed{b}", align_bytes=64) for b in range(B)]
        k_codes = [keep.tile([P, N], U32, name=f"k_codes{b}", align_bytes=64) for b in range(B)]
        k_scales = [keep.tile([P, N], U8, name=f"k_scales{b}", align_bytes=64) for b in range(B)]
        v_rows = [keep.tile([P, B * N], F32, name=f"v_rows{h}") for h in range(VB)]
        v_packed = [keep.tile([P, DV, PACK], BF16, name=f"v_packed{b}", align_bytes=64) for b in range(B)]
        v_codes = [keep.tile([P, DV], U32, name=f"v_codes{b}", align_bytes=64) for b in range(B)]
        v_scales = [keep.tile([P, DV], U8, name=f"v_scales{b}", align_bytes=64) for b in range(B)]
        units = [(b, m) for b in range(B) for m in range(QT)]
        w_codes = {u: keep.tile([P, P], U32, name=f"w_codes{u[0]}{u[1]}", align_bytes=64) for u in units}
        w_scales = {u: keep.tile([P, P], U8, name=f"w_scales{u[0]}{u[1]}", align_bytes=64) for u in units}
        w_packed = {u: keep.tile([P, P, PACK], BF16, name=f"w_packed{u[0]}{u[1]}", align_bytes=64) for u in units}
        th = {u: keep.tile([P, N], F32, name=f"th{u[0]}{u[1]}") for u in units}
        low = {u: keep.tile([P, 1], F32, name=f"low{u[0]}{u[1]}") for u in units}
        p = {u: keep.tile([P, PACK, P], F32, name=f"p{u[0]}{u[1]}") for u in units}
        score, wt, vt, acc = {}, {}, {}, {}
        over = {(0, 1): "v_pool0"}

        def quant(codes, scales, packed):
            nc.vector.quantize_mx(out=codes.bitcast(FP8X4), scales=scales, in_=packed.rearrange("p n j -> p (n j)"))

        def interleave_q(copy, b):
            copy(q_packed[b][:], q_raw[b][:].rearrange("p j n -> p n j"))

        def quant_q(b):
            quant(q_codes[b][:], q_scales[b][:], q_packed[b][:])

        def gather_vs():
            nc.vector.tensor_copy(vs_row[:], vs_pool[:].indirect(offsets[:]))

        def turn_vs():
            for b in range(B):
                up = psum.tile([P, PACK, P], F32, name="turn", bufs=4)
                for t in range(PACK):
                    nc.tensor.transpose(up[:, t, :], vs_row[:, b * N + t : (b + 1) * N : PACK], ident[:])
                nc.scalar.copy(vs_col[:, b, :], up[:, :, 0])

        def gather_k(t):
            nc.vector.tensor_copy(k_rows_of[:, t, :], k_pool[t][:].indirect(offsets[:]))

        def gather_k_of(t, b):
            nc.vector.tensor_copy(k_rows_of[:, t, b * N : (b + 1) * N], k_pool[t][:].indirect(offsets[:, b * COLS : (b + 1) * COLS]))

        def interleave_k(copy, t, b):
            copy(k_packed[b][:, :, t : t + 2], k_rows_of[:, t : t + 2, b * N : (b + 1) * N].rearrange("p j n -> p n j"))

        def quant_k(b):
            quant(k_codes[b][:], k_scales[b][:], k_packed[b][:])

        def scores(b, m):
            cols = slice(m * P, (m + 1) * P)
            s = psum.tile([P, N], F32, name="score", bufs=2)
            score[b, m] = s
            nc.tensor.matmul_mx(
                out=s[:],
                lhsT=q_codes[b][:, cols].bitcast(FP8X4),
                lhsT_scale=q_scales[b][:, cols],
                rhs=k_codes[b][:].bitcast(FP8X4),
                rhs_scale=k_scales[b][:],
                start=True,
                stop=True,
            )

        def squash(*u):
            nc.scalar.activation(th[u][:], score[u][:], ACT.Tanh, scale=1.0 / CAP)

        def lowest(*u):
            if u in over:
                neg = keep.tile([P, N], F32, name=f"neg{u[0]}{u[1]}", tag=over[u])
            else:
                neg = work.tile([P, N], F32, name="neg")
            nc.vector.tensor_scalar(neg[:], th[u][:], -CAP, None, op0=ALU.mult, op1=ALU.min, accum_out=low[u][:])

        def expo(*u):
            i = units.index(u)
            nc.scalar.activation(
                p[u][:].rearrange("q t s -> q s t"),
                th[u][:].rearrange("q (s t) -> q s t", t=PACK),
                ACT.Exp,
                bias=low[u][:],
                scale=CAP,
                accum_out=totals[:, i : i + 1],
            )

        def turn_w(*u):
            x = psum.tile([P, PACK, P], F32, name="turn", bufs=4)
            wt[u] = x
            for t in range(PACK):
                nc.tensor.transpose(x[:, t, :], p[u][:, t, :], ident[:])

        def weigh(*u):
            nc.vector.tensor_tensor(
                w_packed[u][:],
                wt[u][:].rearrange("p t q -> p q t"),
                vs_col[:, u[0], :].unsqueeze(1).to_broadcast([P, P, PACK]),
                ALU.mult,
            )

        def quant_w(*u):
            quant(w_codes[u][:], w_scales[u][:], w_packed[u][:])

        def gather_v(h):
            nc.vector.tensor_copy(v_rows[h][:], v_pool[h][:].indirect(offsets[:]))

        def turn_v(h, b):
            x = psum.tile([P, PACK, P], F32, name="turn", bufs=4)
            vt[h, b] = x
            for t in range(PACK):
                nc.tensor.transpose(x[:, t, :], v_rows[h][:, b * N + t : (b + 1) * N : PACK], ident[:])

        def pack_v(copy, h, b):
            copy(v_packed[b][:, h * P : (h + 1) * P, :], vt[h, b][:].rearrange("p t e -> p e t"))

        def quant_v(b):
            quant(v_codes[b][:], v_scales[b][:], v_packed[b][:])

        def product(*u):
            b = u[0]
            y = psum.tile([P, DV], F32, name="y", bufs=2)
            acc[u] = y
            nc.tensor.matmul_mx(
                out=y[:],
                lhsT=w_codes[u][:].bitcast(FP8X4),
                lhsT_scale=w_scales[u][:],
                rhs=v_codes[b][:].bitcast(FP8X4),
                rhs_scale=v_scales[b][:],
                start=True,
                stop=True,
            )

        def finish(b, m, scalar):
            u = (b, m)
            i = units.index(u)
            y = acc[u]
            res = work.tile([P, DV], F32, name="res")
            if scalar:
                nc.scalar.activation(res[:], y[:], ACT.Copy, scale=inv[:, i : i + 1])
            else:
                nc.vector.tensor_scalar(res[:], y[:], inv[:, i : i + 1], None, op0=ALU.mult)
            nc.sync.dma_start(out[b, m * P : (m + 1) * P, :], res[:])

        nc.gpsimd.memset(vs_pool[:, T // 2 : T], 0.0)
        nc.vector.memset(vs_pool[:, 0 : T // 2], 0.0)
        nc.sync.dma_start(offsets[:], offs)
        k_rows = kT.rearrange("(p j) n -> j p n", j=PACK)
        q_rows = [qT[b].rearrange("(p j) n -> p j n", j=PACK) for b in range(B)]
        nc.sync.dma_start(k_pool[0][:], k_rows[0])
        nc.sync.dma_start(vs_pool[0:1, :], vs[0:1, :])
        nc.sync.dma_start(k_pool[1][:], k_rows[1])
        nc.sync.dma_start(q_raw[0][:], q_rows[0])
        nc.sync.dma_start(k_pool[2][:], k_rows[2])
        nc.sync.dma_start(k_pool[3][:], k_rows[3])
        nc.sync.dma_start(q_raw[1][:], q_rows[1])
        nc.sync.dma_start(v_pool[0][:], vT[0:128, :])
        nc.sync.dma_start(v_pool[1][:], vT[128:256, :])
        nc.vector.memset(warm[:], 0.0)
        nc.scalar.activation(warm[:], warm[:], ACT.Exp)
        make_identity(nc, ident[:])

        gather_v(0)
        gather_v(1)
        gather_k(0)
        gather_k(2)
        gather_k(1)
        gather_vs()
        gather_k_of(3, 0)
        interleave_k(nc.scalar.copy, 0, 0)
        interleave_q(nc.vector.tensor_copy, 0)
        gather_k_of(3, 1)
        interleave_k(nc.vector.tensor_copy, 2, 1)
        quant_q(0)
        interleave_k(nc.vector.tensor_copy, 2, 0)
        quant_k(0)
        scores(0,1)
        interleave_q(nc.scalar.copy, 1)
        turn_vs()
        interleave_k(nc.vector.tensor_copy, 0, 1)
        turn_v(0,0)
        squash(0,1)
        quant_q(1)
        scores(0,0)
        squash(0,0)
        lowest(0,0)
        quant_k(1)
        scores(1,0)
        expo(0,0)
        pack_v(nc.scalar.copy, 0, 0)
        lowest(0,1)
        expo(0,1)
        squash(1,0)
        lowest(1,0)
        turn_v(0,1)
        expo(1,0)
        scores(1,1)
        squash(1,1)
        lowest(1,1)
        pack_v(nc.scalar.copy, 0, 1)
        turn_w(0,0)
        turn_v(1,0)
        expo(1,1)
        turn_w(0,1)
        nc.vector.reciprocal(inv[:], totals[:])
        turn_w(1,1)
        weigh(0,0)
        pack_v(nc.scalar.copy, 1, 0)
        turn_v(1,1)
        quant_w(0,0)
        quant_v(0)
        pack_v(nc.scalar.copy, 1, 1)
        weigh(0,1)
        quant_w(0,1)
        turn_w(1,0)
        weigh(1,1)
        weigh(1,0)
        product(0,1)
        product(0,0)
        quant_w(1,1)
        finish(0, 0, True)
        quant_v(1)
        finish(0, 1, True)
        product(1,1)
        quant_w(1,0)
        product(1,0)
        finish(1, 0, True)
        finish(1, 1, False)
